import numpy as np, ml_dtypes
CORES = [16,32,48,64,80]
N = 5
import mx_ref
NC = 128
BF = ml_dtypes.bfloat16
def setup_inputs(rng):
    def f(*shape):
        return mx_ref.flush((rng.standard_normal(shape, dtype=np.float32) * np.exp2(rng.integers(-2, 3, shape[:-1] + (1,)))).astype(BF))
    return {"v": f(N, 128, 512), "p": f(N, 128, N * 4 * NC)}
def setup_inputs_blocks(rng):
    d = setup_inputs(rng)
    for k in ("v", "p"): d[k] = mx_ref.spread(d[k], rng, 2)
    return d
def setup_inputs_wide(rng):
    d = setup_inputs(rng)
    for k in ("v", "p"): d[k] = mx_ref.flush((d[k].astype(np.float32) * np.exp2(rng.integers(-8, 9, (N, 1, 1))).astype(np.float32)).astype(BF))
    return d
def setup_inputs_zeros(rng):
    d = setup_inputs(rng); v = d["p"].reshape(N, 128, -1, 4).copy()
    v[np.broadcast_to((rng.random((N, 1, v.shape[2], 1)) < 0.33), v.shape)] = 0
    d["p"] = v.reshape(d["p"].shape)
    return d
def reference(v, p):
    QV = [mx_ref.quantize(v[j]) for j in range(N)]
    y = np.zeros((N, 128, NC), np.float32)
    for r in range(N):
        for j in range(N):
            s = mx_ref.matmul(QV[j], mx_ref.quantize(p[r][:, 4 * NC * j:4 * NC * j + 4 * NC]))
            y[r] = s if j == 0 else y[r] + s
    return {"y": y}

@@ -1,0 +1,116 @@
+from concourse.bass import DstId, RemoteDMATransfer
+from concourse.mybir import dt
+
+N = 5
+COLS = 128
+ELEMS = 4 * COLS
+NSIM = 96
+VIA_HELPER = (3, 4)
+
+SCRATCH = {
+    "vb": ("sbuf", [128, ELEMS], "bfloat16"),
+    "pb": ("sbuf", [128, N * ELEMS], "bfloat16"),
+    "vq": ("sbuf", [128, N * COLS], "float8_e4m3fn_x4"),
+    "vs": ("sbuf", [128, N * COLS], "uint8"),
+    "pq": ("sbuf", [128, N * COLS], "float8_e4m3fn_x4"),
+    "ps": ("sbuf", [128, N * COLS], "uint8"),
+    "acc": ("psum", [128, 512], "float32"),
+    "yb": ("sbuf", [128, COLS], "float32"),
+}
+SEMAPHORES = ["vld", "pld", "qv", "qp", "mm", "cp", "st", "sent", "hs", "hc"] + ["arr%d" % j for j in range(N)]
+
+
+def _helper_of(c, T, topo):
+    for x in range(NSIM):
+        if (topo.chip(x) == topo.chip(c) and topo.die(x) != topo.die(c) and T.rank_of(x) is None
+                and all(topo.may_write(x, d) for d in T.cores if d != c)):
+            return x
+    return None
+
+
+def _engines(topo, src, dsts):
+    m = topo.mask(src, dsts[0])
+    for d in dsts[1:]:
+        m &= topo.mask(src, d)
+    return m
+
+
+def _copy(g, topo, dsts, view, mask, remote_sem, local_sem):
+    ids = []
+    for d in dsts:
+        rid, pid, _ring = topo.addr(d)
+        ids.append(DstId(rid=rid, pnc=pid))
+    g.remote_dma_fused([RemoteDMATransfer(dst_ids=ids, dma_engine_mask=mask, remote_sem=remote_sem,
+                                          srcs=[view], dsts=[view for _d in dsts])], local_sem=local_sem)
+    return bin(mask).count("1")
+
+
+def _helper_program(g, core, T, topo, r):
+    S = T.sem
+    sl = slice(COLS * r, COLS * (r + 1))
+    far = [T.cores[(r + k) % N] for k in VIA_HELPER]
+    got = bin(_engines(topo, T.cores[r], [core] + [d for d in T.cores if d != T.cores[r]])).count("1")
+    mask = _engines(topo, core, far)
+    g.wait_ge(S.hs, got)
+    left = _copy(g, topo, far, T.vs[:, sl], mask, S["arr%d" % r], S.sent)
+    g.wait_ge(S.hc, got)
+    left += _copy(g, topo, far, T.vq[:, sl].bitcast(dt.uint8), mask, S["arr%d" % r], S.sent)
+    g.wait_ge(S.sent, left)
+
+
+def rank_program(g, core, T, topo):
+    r = T.rank_of(core)
+    if r is None:
+        for j, c in enumerate(T.cores):
+            if VIA_HELPER and _helper_of(c, T, topo) == core:
+                _helper_program(g, core, T, topo, j)
+        return
+    S = T.sem
+    own = slice(COLS * r, COLS * (r + 1))
+
+    g.sync.dma_start(T.vb[:], T.v[:]).then_inc(S.vld, 16)
+    g.sync.dma_start(T.pb[:], T.p[:]).then_inc(S.pld, 16)
+
+    g.vector.wait_ge(S.vld, 16)
+    g.vector.quantize_mx(T.vq[:, own], T.vs[:, own], T.vb[:]).then_inc(S.qv, 1)
+    g.vector.wait_ge(S.pld, 16)
+    for j in range(N):
+        sl = slice(COLS * j, COLS * (j + 1))
+        g.vector.quantize_mx(T.pq[:, sl], T.ps[:, sl], T.pb[:, ELEMS * j:ELEMS * (j + 1)]).then_inc(S.qp, 1)
+
+    near = [T.cores[(r + k) % N] for k in range(1, N) if k not in VIA_HELPER]
+    helper = _helper_of(core, T, topo) if VIA_HELPER else None
+    mask = _engines(topo, core, ([helper] if VIA_HELPER else []) + [d for d in T.cores if d != core])
+    codes = T.vq[:, own].bitcast(dt.uint8)
+    plane = T.vs[:, own]
+    left = 0
+    g.wait_ge(S.qv, 1)
+    if VIA_HELPER:
+        left += _copy(g, topo, [helper], plane, mask, S.hs, S.sent)
+        left += _copy(g, topo, [helper], codes, mask, S.hc, S.sent)
+    left += _copy(g, topo, near, plane, mask, S["arr%d" % r], S.sent)
+    left += _copy(g, topo, near, codes, mask, S["arr%d" % r], S.sent)
+
+    out = T.acc[:, 0:COLS]
+    g.tensor.wait_ge(S.qv, 1)
+    g.tensor.wait_ge(S.qp, N)
+    g.tensor.matmul_mx(out, T.vq[:, own], T.vs[:, own], T.pq[:, own], T.ps[:, own], True, False)
+    order = [k for k in range(1, N) if k not in VIA_HELPER] + list(VIA_HELPER)
+    for i, k in enumerate(order):
+        j = (r - k) % N
+        src = _helper_of(T.cores[j], T, topo) if k in VIA_HELPER else T.cores[j]
+        if k in VIA_HELPER:
+            n = bin(_engines(topo, src, [T.cores[(j + q) % N] for q in VIA_HELPER])).count("1")
+        else:
+            n = bin(mask).count("1")
+        sl = slice(COLS * j, COLS * (j + 1))
+        g.tensor.wait_ge(S["arr%d" % j], 2 * n)
+        mm = g.tensor.matmul_mx(out, T.vq[:, sl], T.vs[:, sl], T.pq[:, sl], T.ps[:, sl], False, i == N - 2)
+    mm.then_inc(S.mm, 1)
+
+    g.vector.wait_ge(S.mm, 1)
+    g.vector.tensor_copy(T.yb[:], out).then_inc(S.cp, 1)
+    g.sync.wait_ge(S.cp, 1)
+    g.sync.dma_start(T.y[:], T.yb[:]).then_inc(S.st, 16)
+    g.sync.wait_ge(S.st, 16)
+    g.wait_ge(S.sent, left)

@@ -5,7 +5,9 @@ N = 5
 COLS = 128
 ELEMS = 4 * COLS
 NSIM = 96
-VIA_HELPER = (3, 4)
+DIRECT = (1, 2, 3)
+RELAYED = (4,)
+HOP_ENGINES = 4
 
 SCRATCH = {
     "vb": ("sbuf", [128, ELEMS], "bfloat16"),
@@ -35,6 +37,11 @@ def _engines(topo, src, dsts):
     return m
 
 
+def _some(mask, n):
+    b = [x for x in range(mask.bit_length()) if (mask >> x) & 1]
+    return sum(1 << x for x in b[::len(b) // n][:n])
+
+
 def _copy(g, topo, dsts, view, mask, remote_sem, local_sem):
     ids = []
     for d in dsts:
@@ -48,12 +55,11 @@ def _copy(g, topo, dsts, view, mask, remote_sem, local_sem):
 def _helper_program(g, core, T, topo, r):
     S = T.sem
     sl = slice(COLS * r, COLS * (r + 1))
-    far = [T.cores[(r + k) % N] for k in VIA_HELPER]
-    got = bin(_engines(topo, T.cores[r], [core] + [d for d in T.cores if d != T.cores[r]])).count("1")
+    far = [T.cores[(r + k) % N] for k in RELAYED]
     mask = _engines(topo, core, far)
-    g.wait_ge(S.hs, got)
+    g.wait_ge(S.hs, HOP_ENGINES)
     left = _copy(g, topo, far, T.vs[:, sl], mask, S["arr%d" % r], S.sent)
-    g.wait_ge(S.hc, got)
+    g.wait_ge(S.hc, HOP_ENGINES)
     left += _copy(g, topo, far, T.vq[:, sl].bitcast(dt.uint8), mask, S["arr%d" % r], S.sent)
     g.wait_ge(S.sent, left)
 
@@ -62,7 +68,7 @@ def rank_program(g, core, T, topo):
     r = T.rank_of(core)
     if r is None:
         for j, c in enumerate(T.cores):
-            if VIA_HELPER and _helper_of(c, T, topo) == core:
+            if _helper_of(c, T, topo) == core:
                 _helper_program(g, core, T, topo, j)
         return
     S = T.sem
@@ -78,34 +84,31 @@ def rank_program(g, core, T, topo):
         sl = slice(COLS * j, COLS * (j + 1))
         g.vector.quantize_mx(T.pq[:, sl], T.ps[:, sl], T.pb[:, ELEMS * j:ELEMS * (j + 1)]).then_inc(S.qp, 1)
 
-    near = [T.cores[(r + k) % N] for k in range(1, N) if k not in VIA_HELPER]
-    helper = _helper_of(core, T, topo) if VIA_HELPER else None
-    mask = _engines(topo, core, ([helper] if VIA_HELPER else []) + [d for d in T.cores if d != core])
+    near = [T.cores[(r + k) % N] for k in DIRECT]
+    helper = _helper_of(core, T, topo)
+    off = _engines(topo, core, near)
+    hop = _some(topo.mask(core, helper) & ~off, HOP_ENGINES)
     codes = T.vq[:, own].bitcast(dt.uint8)
     plane = T.vs[:, own]
-    left = 0
+    mine = S["arr%d" % r]
     g.wait_ge(S.qv, 1)
-    if VIA_HELPER:
-        left += _copy(g, topo, [helper], plane, mask, S.hs, S.sent)
-        left += _copy(g, topo, [helper], codes, mask, S.hc, S.sent)
-    left += _copy(g, topo, near, plane, mask, S["arr%d" % r], S.sent)
-    left += _copy(g, topo, near, codes, mask, S["arr%d" % r], S.sent)
+    left = _copy(g, topo, [helper], plane, hop, S.hs, S.sent)
+    left += _copy(g, topo, near, plane, off, mine, S.sent)
+    left += _copy(g, topo, [helper], codes, hop, S.hc, S.sent)
+    for d in near:
+        left += _copy(g, topo, [d], codes, off, mine, S.sent)
 
     out = T.acc[:, 0:COLS]
     g.tensor.wait_ge(S.qv, 1)
     g.tensor.wait_ge(S.qp, N)
     g.tensor.matmul_mx(out, T.vq[:, own], T.vs[:, own], T.pq[:, own], T.ps[:, own], True, False)
-    order = [k for k in range(1, N) if k not in VIA_HELPER] + list(VIA_HELPER)
-    for i, k in enumerate(order):
+    for k in DIRECT + RELAYED:
         j = (r - k) % N
-        src = _helper_of(T.cores[j], T, topo) if k in VIA_HELPER else T.cores[j]
-        if k in VIA_HELPER:
-            n = bin(_engines(topo, src, [T.cores[(j + q) % N] for q in VIA_HELPER])).count("1")
-        else:
-            n = bin(mask).count("1")
         sl = slice(COLS * j, COLS * (j + 1))
+        src = _helper_of(T.cores[j], T, topo) if k in RELAYED else T.cores[j]
+        n = bin(_engines(topo, src, [core])).count("1")
         g.tensor.wait_ge(S["arr%d" % j], 2 * n)
-        mm = g.tensor.matmul_mx(out, T.vq[:, sl], T.vs[:, sl], T.pq[:, sl], T.ps[:, sl], False, i == N - 2)
+        mm = g.tensor.matmul_mx(out, T.vq[:, sl], T.vs[:, sl], T.pq[:, sl], T.ps[:, sl], False, k == RELAYED[-1])
     mm.then_inc(S.mm, 1)
 
     g.vector.wait_ge(S.mm, 1)

from concourse.bass import DstId, RemoteDMATransfer
from concourse.mybir import dt

N = 5
COLS = 128
ELEMS = 4 * COLS
NSIM = 96
DIRECT = (1, 2, 3)
RELAYED = (4,)
HOP_ENGINES = 4

SCRATCH = {
    "vb": ("sbuf", [128, ELEMS], "bfloat16"),
    "pb": ("sbuf", [128, N * ELEMS], "bfloat16"),
    "vq": ("sbuf", [128, N * COLS], "float8_e4m3fn_x4"),
    "vs": ("sbuf", [128, N * COLS], "uint8"),
    "pq": ("sbuf", [128, N * COLS], "float8_e4m3fn_x4"),
    "ps": ("sbuf", [128, N * COLS], "uint8"),
    "acc": ("psum", [128, 512], "float32"),
    "yb": ("sbuf", [128, COLS], "float32"),
}
SEMAPHORES = ["vld", "pld", "qv", "qp", "mm", "cp", "st", "sent", "hs", "hc"] + ["arr%d" % j for j in range(N)]


def _helper_of(c, T, topo):
    for x in range(NSIM):
        if (topo.chip(x) == topo.chip(c) and topo.die(x) != topo.die(c) and T.rank_of(x) is None
                and all(topo.may_write(x, d) for d in T.cores if d != c)):
            return x
    return None


def _engines(topo, src, dsts):
    m = topo.mask(src, dsts[0])
    for d in dsts[1:]:
        m &= topo.mask(src, d)
    return m


def _some(mask, n):
    b = [x for x in range(mask.bit_length()) if (mask >> x) & 1]
    return sum(1 << x for x in b[::len(b) // n][:n])


def _copy(g, topo, dsts, view, mask, remote_sem, local_sem):
    ids = []
    for d in dsts:
        rid, pid, _ring = topo.addr(d)
        ids.append(DstId(rid=rid, pnc=pid))
    g.remote_dma_fused([RemoteDMATransfer(dst_ids=ids, dma_engine_mask=mask, remote_sem=remote_sem,
                                          srcs=[view], dsts=[view for _d in dsts])], local_sem=local_sem)
    return bin(mask).count("1")


def _helper_program(g, core, T, topo, r):
    S = T.sem
    sl = slice(COLS * r, COLS * (r + 1))
    far = [T.cores[(r + k) % N] for k in RELAYED]
    mask = _engines(topo, core, far)
    g.wait_ge(S.hs, HOP_ENGINES)
    left = _copy(g, topo, far, T.vs[:, sl], mask, S["arr%d" % r], S.sent)
    g.wait_ge(S.hc, HOP_ENGINES)
    left += _copy(g, topo, far, T.vq[:, sl].bitcast(dt.uint8), mask, S["arr%d" % r], S.sent)
    g.wait_ge(S.sent, left)


def rank_program(g, core, T, topo):
    r = T.rank_of(core)
    if r is None:
        for j, c in enumerate(T.cores):
            if _helper_of(c, T, topo) == core:
                _helper_program(g, core, T, topo, j)
        return
    S = T.sem
    own = slice(COLS * r, COLS * (r + 1))

    g.sync.dma_start(T.vb[:], T.v[:]).then_inc(S.vld, 16)
    g.sync.dma_start(T.pb[:], T.p[:]).then_inc(S.pld, 16)

    g.vector.wait_ge(S.vld, 16)
    g.vector.quantize_mx(T.vq[:, own], T.vs[:, own], T.vb[:]).then_inc(S.qv, 1)
    g.vector.wait_ge(S.pld, 16)
    for j in range(N):
        sl = slice(COLS * j, COLS * (j + 1))
        g.vector.quantize_mx(T.pq[:, sl], T.ps[:, sl], T.pb[:, ELEMS * j:ELEMS * (j + 1)]).then_inc(S.qp, 1)

    near = [T.cores[(r + k) % N] for k in DIRECT]
    helper = _helper_of(core, T, topo)
    off = _engines(topo, core, near)
    hop = _some(topo.mask(core, helper) & ~off, HOP_ENGINES)
    codes = T.vq[:, own].bitcast(dt.uint8)
    plane = T.vs[:, own]
    mine = S["arr%d" % r]
    g.wait_ge(S.qv, 1)
    left = _copy(g, topo, [helper], plane, hop, S.hs, S.sent)
    left += _copy(g, topo, near, plane, off, mine, S.sent)
    left += _copy(g, topo, [helper], codes, hop, S.hc, S.sent)
    for d in near:
        left += _copy(g, topo, [d], codes, off, mine, S.sent)

    out = T.acc[:, 0:COLS]
    g.tensor.wait_ge(S.qv, 1)
    g.tensor.wait_ge(S.qp, N)
    g.tensor.matmul_mx(out, T.vq[:, own], T.vs[:, own], T.pq[:, own], T.ps[:, own], True, False)
    for k in DIRECT + RELAYED:
        j = (r - k) % N
        sl = slice(COLS * j, COLS * (j + 1))
        src = _helper_of(T.cores[j], T, topo) if k in RELAYED else T.cores[j]
        n = bin(_engines(topo, src, [core])).count("1")
        g.tensor.wait_ge(S["arr%d" % j], 2 * n)
        mm = g.tensor.matmul_mx(out, T.vq[:, sl], T.vs[:, sl], T.pq[:, sl], T.ps[:, sl], False, k == RELAYED[-1])
    mm.then_inc(S.mm, 1)

    g.vector.wait_ge(S.mm, 1)
    g.vector.tensor_copy(T.yb[:], out).then_inc(S.cp, 1)
    g.sync.wait_ge(S.cp, 1)
    g.sync.dma_start(T.y[:], T.yb[:]).then_inc(S.st, 16)
    g.sync.wait_ge(S.st, 16)
    g.wait_ge(S.sent, left)
